import numpy as np
import ml_dtypes


def mxq(x, axis, fmt="e4m3"):
    dtype, down = {"e4m3": (ml_dtypes.float8_e4m3fn, 7), "e5m2": (ml_dtypes.float8_e5m2, 14)}[fmt]
    v = np.moveaxis(np.asarray(x, np.float32).astype(ml_dtypes.bfloat16).astype(np.float64), axis, -1)
    blocks = v.reshape(v.shape[:-1] + (-1, 32))
    amax = np.abs(blocks).max(-1, keepdims=True)
    byte = np.maximum(np.where(amax > 0, np.frexp(amax)[1] - 1 + 127, 0) - down, 1)
    scale = np.exp2(byte - 127.0)
    codes = (blocks / scale).astype(np.float32).astype(dtype).astype(np.float64)
    return np.moveaxis((codes * scale).reshape(v.shape), -1, axis)


WIDE = False


def mx_kscale(k):
    if not WIDE:
        return np.ones(k)
    levels = np.array([10, -10, 5, -5, 0])
    if k % 512:
        return np.exp2(np.random.permutation(np.resize(levels, k // 32))).repeat(32)
    a = np.empty((k // 512, 16))
    for p in range(k // 512):
        a[p, :8] = np.random.permutation(np.resize(levels, 8))
        for g in range(8):
            far = levels[np.abs(levels - a[p, g]) >= 10]
            a[p, g + 8] = far[np.random.randint(len(far))]
    return np.exp2(a.ravel()).repeat(32)


def f64(x):
    return np.asarray(x).astype(np.float64)


def striped(idx):
    return np.tile(idx.reshape(-1, 16).T, (8, 1)).astype(np.uint16)


def unstriped(offs):
    return offs[:16].T.reshape(-1).astype(np.int64)


def pack_weight(w):
    k, n = w.shape
    w = f64(np.asarray(w, np.float32).astype(ml_dtypes.bfloat16)).reshape(k // 32, 32, n)
    amax = np.abs(w).max(1)
    byte = np.clip(np.where(amax > 0, np.frexp(amax)[1] - 1 + 127 - 7, 1), 1, 254)
    scaled = (w * np.exp2(127.0 - byte)[:, None, :]).reshape(k, n).astype(np.float32)
    words = np.ascontiguousarray(scaled.reshape(k // 512, 128, 4, n).transpose(0, 1, 3, 2)).astype(ml_dtypes.float8_e4m3fn).view(np.uint8)
    return words, np.ascontiguousarray(byte.astype(np.uint8).reshape(k // 512, 16, n))


def unpack_weight(words, scales):
    g, p, n, _ = words.shape
    vals = np.ascontiguousarray(words).view(ml_dtypes.float8_e4m3fn).astype(np.float64) * np.repeat(np.exp2(scales.astype(np.float64) - 127.0), 8, axis=1)[..., None]
    return vals.transpose(0, 1, 3, 2).reshape(g * 512, n)


E2M1 = np.array([0.0, 0.5, 1.0, 1.5, 2.0, 3.0, 4.0, 6.0, -0.0, -0.5, -1.0, -1.5, -2.0, -3.0, -4.0, -6.0])


def pack_fp4(w):
    k, n = w.shape
    w = f64(np.asarray(w, np.float32).astype(ml_dtypes.bfloat16)).reshape(k // 32, 32, n)
    amax = np.abs(w).max(1)
    mant, ex = np.frexp(amax / 6.0)
    byte = np.clip(np.where(amax > 0, np.where(mant > 0.5, ex, ex - 1) + 127, 1), 1, 254)
    scaled = (w * np.exp2(127.0 - byte)[:, None, :]).reshape(k, n).astype(np.float32)
    c = np.ascontiguousarray(scaled.reshape(k // 512, 128, 4, n).transpose(0, 1, 3, 2)).astype(ml_dtypes.float4_e2m1fn).view(np.uint8) & 0xF
    words = (c[..., 0::2] | (c[..., 1::2] << 4)).reshape(k // 512, 128, 2 * n)
    return np.ascontiguousarray(words), np.ascontiguousarray(byte.astype(np.uint8).reshape(k // 512, 16, n))


def unpack_fp4(words, scales):
    g, _, n = scales.shape
    words = np.ascontiguousarray(words).reshape(g, 128, n, 2)
    nib = np.empty((g, 128, n, 4), np.uint8)
    nib[..., 0::2] = words & 0xF
    nib[..., 1::2] = words >> 4
    vals = E2M1[nib] * np.repeat(np.exp2(scales.astype(np.float64) - 127.0), 8, axis=1)[..., None]
    return vals.transpose(0, 1, 3, 2).reshape(g * 512, n)


def planes(y):
    n, m = y.shape
    v = y.astype(np.float32).astype(ml_dtypes.bfloat16).astype(np.float64).reshape(n // 32, 32, m)
    top = np.abs(v).max(1)
    byte = np.clip(np.where(top > 0, np.frexp(top)[1] - 1 + 127 - 7, 1), 1, 254)
    codes = (v * np.exp2(127.0 - byte)[:, None, :]).reshape(n, m).astype(np.float32).astype(ml_dtypes.float8_e4m3fn).view(np.uint8)
    words = codes.reshape(n // 512, 128, 4, m).transpose(0, 1, 3, 2)
    return np.ascontiguousarray(words), np.ascontiguousarray(byte.astype(np.uint8).reshape(n // 512, 16, m))


K, T, S, N, H, U = 1024, 2048, 512, 512, 512, 1024


def setup_inputs():
    n = np.random.standard_normal
    s = mx_kscale(K)[:, None]
    u = mx_kscale(H)
    packed_xT = pack_weight(n((K, T)) * s)
    packed_w1 = pack_fp4(n((K, N)) / np.sqrt(K) / s)
    packed_w2 = pack_fp4(n((K, N)) / np.sqrt(K) / s)
    packed_w3 = pack_fp4(n((H, N)) / np.sqrt(H) / u[:, None])
    return {
        "x_words": packed_xT[0],
        "x_scales": packed_xT[1],
        "w1_words": packed_w1[0],
        "w1_scales": packed_w1[1],
        "w2_words": packed_w2[0],
        "w2_scales": packed_w2[1],
        "unit": (np.random.uniform(0.6, 1.4, (H, 1)) * u[:, None]).astype(np.float32),
        "w3_words": packed_w3[0],
        "w3_scales": packed_w3[1],
        "offs": striped(np.random.permutation(T)[:S]),
        "l1": striped(np.random.permutation(np.concatenate([np.arange(S), np.random.randint(0, S, U - S)]))),
        "r1": striped(np.random.permutation(np.concatenate([np.arange(S), np.random.randint(0, S, U - S)]))),
    }


def reference(x_words, x_scales, w1_words, w1_scales, w2_words, w2_scales, unit, w3_words, w3_scales, offs, l1, r1):
    xq = unpack_weight(x_words, x_scales)[:, unstriped(offs)]
    y = unpack_fp4(w1_words, w1_scales).T @ xq
    yl = y[:, unstriped(l1)]
    yr = y[:, unstriped(r1)]
    sim = yl * yr
    z1 = unpack_fp4(w2_words, w2_scales).T @ xq
    zl = z1[:, unstriped(l1)]
    zr = z1[:, unstriped(r1)]
    hid = f64(unit) * (np.maximum(sim, zl) - np.minimum(sim, zr))
    out_0 = unpack_fp4(w3_words, w3_scales).T @ mxq(hid, 0, "e4m3")
    return (out_0,) + planes(out_0)

@@ -1,0 +1,229 @@
+from contextlib import ExitStack
+
+import concourse.mybir as mybir
+
+K, T, S, N, H, U = 1024, 2048, 512, 512, 512, 1024
+FLOPS = 2 * (2 * K * N * S + H * N * U)
+
+F32 = mybir.dt.float32
+BF16 = mybir.dt.bfloat16
+I32 = mybir.dt.int32
+U32 = mybir.dt.uint32
+U16 = mybir.dt.uint16
+U8 = mybir.dt.uint8
+FP8X4 = mybir.dt.float8_e4m3fn_x4
+FP4X4 = mybir.dt.float4_e2m1fn_x4
+ALU = mybir.AluOpType
+COPY = mybir.ActivationFunctionType.Copy
+
+P = 128
+PACK = 4
+PASSES = K // (P * PACK)
+QUADS = 4
+SPARE = 16
+CHUNKS = (256, 512, 256)
+BLOCK = 128
+STRIP = 256
+
+
+def tile_picked_ysegmrg_rng_po_kernel(
+    tc, x_words, x_scales, w1_words, w1_scales, w2_words, w2_scales, unit, w3_words, w3_scales, offs, l1, r1,
+    out_0, out_1, out_2,
+):
+    nc = tc.nc
+    with ExitStack() as ctx:
+        keep = ctx.enter_context(tc.tile_pool(name="keep", bufs=1))
+        ring = ctx.enter_context(tc.tile_pool(name="ring", bufs=3))
+        psum = ctx.enter_context(tc.psum_pool(name="psum", bufs=8))
+
+        def load_scale_rows(queue, tile, scales):
+            for q in range(QUADS):
+                queue.dma_start(
+                    out=tile[32 * q : 32 * q + 4].bitcast(I32),
+                    in_=scales[:, 4 * q : 4 * q + 4, :].rearrange("g a c -> a g c").bitcast(I32),
+                )
+
+        def zeroed_plane(engine, name, passes, width):
+            tile = keep.tile([P, passes, width], U8, name=name, align_bytes=64)
+            engine.memset(tile[:].bitcast(I32), 0)
+            return tile
+
+        def load_words(queue, name, words):
+            passes = words.shape[0]
+            tile = keep.tile([P, passes, 2 * N], U8, name=name, align_bytes=64)
+            queue.dma_start(out=tile[:].bitcast(I32), in_=words.rearrange("g p b -> p g b").bitcast(I32))
+            return tile
+
+        def deal(name, raw_words, raw_scales):
+            passes = raw_words.shape[1]
+            words = keep.tile([P, passes, 2 * N], U8, name=name + "_words", align_bytes=64)
+            scales = keep.tile([P, passes, N], U8, name=name + "_scales", align_bytes=64)
+            nc.vector.tensor_copy(
+                out=words[:].bitcast(U16).rearrange("p g (t m) -> p g m t", t=PACK),
+                in_=raw_words[:].bitcast(U16).rearrange("p g (m t) -> p g m t", t=PACK),
+            )
+            nc.vector.tensor_copy(
+                out=scales[:].rearrange("p g (t m) -> p g m t", t=PACK),
+                in_=raw_scales[:].rearrange("p g (m t) -> p g m t", t=PACK),
+            )
+            return words, scales
+
+        def load_list(name, source):
+            tile = keep.tile([P, source.shape[1]], U16, name=name)
+            nc.sync.dma_start(tile[:], source)
+            return tile
+
+        xs_raw = keep.tile([P, T], U8, name="xs_raw", align_bytes=64)
+        nc.vector.memset(xs_raw[:].bitcast(I32), 0)
+        w1s_raw = zeroed_plane(nc.vector, "w1s_raw", PASSES, N)
+        w2s_raw = zeroed_plane(nc.gpsimd, "w2s_raw", PASSES, N)
+        w3s_raw = zeroed_plane(nc.gpsimd, "w3s_raw", 1, N)
+        shifted = zeroed_plane(nc.vector, "shifted", 1, S)
+        for q in range(QUADS):
+            nc.scalar.dma_start(
+                out=xs_raw[32 * q : 32 * q + 4 * PASSES, :].bitcast(I32),
+                in_=x_scales[:, 4 * q : 4 * q + 4, :].bitcast(I32),
+            )
+        load_scale_rows(nc.scalar, w1s_raw, w1_scales)
+        picks = load_list("picks", offs)
+        w1w_raw = load_words(nc.sync, "w1w_raw", w1_words)
+        left = load_list("left", l1)
+        right = load_list("right", r1)
+        xw_raw = [keep.tile([P, T], I32, name="xw_raw%d" % g, align_bytes=64) for g in range(PASSES)]
+        nc.sync.dma_start(out=xw_raw[0][:], in_=x_words[0].rearrange("p c r -> p (c r)").bitcast(I32))
+        w2w_raw = load_words(nc.sync, "w2w_raw", w2_words)
+        nc.sync.dma_start(out=xw_raw[1][:], in_=x_words[1].rearrange("p c r -> p (c r)").bitcast(I32))
+        w3w_raw = load_words(nc.sync, "w3w_raw", w3_words)
+        load_scale_rows(nc.gpsimd, w2s_raw, w2_scales)
+        gain = keep.tile([P, PACK], F32, name="gain")
+        nc.gpsimd.dma_start(out=gain[:], in_=unit.rearrange("(p t) o -> p (t o)", t=PACK))
+        load_scale_rows(nc.gpsimd, w3s_raw, w3_scales)
+
+        y = [keep.tile([P, S + SPARE], F32, name="y%d" % t) for t in range(PACK)]
+        negz = [keep.tile([P, S + SPARE], F32, name="negz%d" % t) for t in range(PACK)]
+        for window in y + negz:
+            nc.vector.memset(window[:, S:], 0.0)
+
+        packed = keep.tile([P, S], U8, name="packed", align_bytes=64)
+        nc.vector.tensor_copy(out=packed[:], in_=xs_raw[:].indirect(picks[:]))
+        nc.sync.dma_start(out=shifted[0:112, 0, :].bitcast(I32), in_=packed[4:116, :].bitcast(I32))
+        xq_scales = [packed[:], shifted[:, 0, :]]
+        xq_words = [keep.tile([P, S], U32, name="xq_words%d" % g, align_bytes=64) for g in range(PASSES)]
+        nc.vector.tensor_copy(out=xq_words[0][:], in_=xw_raw[0][:].bitcast(U32).indirect(picks[:]))
+        w1 = deal("w1", w1w_raw, w1s_raw)
+        nc.vector.tensor_copy(out=xq_words[1][:], in_=xw_raw[1][:].bitcast(U32).indirect(picks[:]))
+        w2 = deal("w2", w2w_raw, w2s_raw)
+        w3 = deal("w3", w3w_raw, w3s_raw)
+
+        def weight_operands(weight, g, t):
+            words, scales = weight
+            return words[:, g, 2 * P * t : 2 * P * (t + 1)].bitcast(FP4X4), scales[:, g, P * t : P * (t + 1)]
+
+        def project(weight, t, window, sign):
+            bank = psum.tile([P, S], F32, name="bank")
+            for g in range(PASSES):
+                lhsT, lhsT_scale = weight_operands(weight, g, t)
+                nc.tensor.matmul_mx(
+                    out=bank[:], lhsT=lhsT, lhsT_scale=lhsT_scale,
+                    rhs=xq_words[g][:].bitcast(FP8X4), rhs_scale=xq_scales[g],
+                    start=(g == 0), stop=(g == PASSES - 1),
+                )
+            nc.scalar.activation(window[:, :S], bank[:], COPY, scale=sign)
+
+        out_rows = out_0.rearrange("(p t) r -> p t r", t=PACK)
+        out_words = out_1[0].rearrange("p c r -> p (c r)").bitcast(I32)
+        out_plane = keep.tile([P, U], U8, name="out_plane", align_bytes=64)
+
+        def fetch(c0, n, t):
+            lo, hi = c0 // 16, (c0 + n) // 16
+            yl = ring.tile([P, n], F32, name="yl")
+            nc.scalar.activation(yl[:], y[t][:].indirect(left[:, lo:hi]), COPY)
+            negzl = ring.tile([P, n], F32, name="negzl")
+            nc.scalar.activation(negzl[:], negz[t][:].indirect(left[:, lo:hi]), COPY)
+            sim = ring.tile([P, n], F32, name="sim")
+            nc.vector.tensor_tensor(sim[:], y[t][:].indirect(right[:, lo:hi]), yl[:], ALU.mult)
+            return sim, negzl
+
+        def differences(c0, n, t, sim, negzl):
+            lo, hi = c0 // 16, (c0 + n) // 16
+            diff = ring.tile([P, 2, n], F32, name="diff")
+            nc.vector.tensor_tensor(diff[:, 0, :], negz[t][:].indirect(right[:, lo:hi]), sim[:], ALU.add)
+            nc.vector.scalar_tensor_tensor(diff[:, 1, :], negzl[:], -1.0, sim[:], ALU.mult, ALU.subtract)
+            return diff
+
+        def clip(t, diff, terms):
+            nc.vector.tensor_scalar(terms[:, :, t, :], diff[:], 0.0, gain[:, t : t + 1], ALU.max, ALU.mult)
+
+        def hidden(terms, s0):
+            cols = slice(s0, s0 + STRIP)
+            hid = ring.tile([P, STRIP, PACK], BF16, name="hid", align_bytes=64)
+            nc.vector.tensor_tensor(
+                hid[:].rearrange("p (c i) t -> p c t i", i=4),
+                terms[:, 0, :, cols].rearrange("p t (c i) -> p c t i", i=4),
+                terms[:, 1, :, cols].rearrange("p t (c i) -> p c t i", i=4),
+                ALU.add,
+            )
+            return hid
+
+        def last_product(hid, r0):
+            codes = ring.tile([P, STRIP], U32, name="hid_codes", align_bytes=64)
+            plane = ring.tile([P, STRIP], U8, name="hid_plane", align_bytes=64)
+            nc.vector.quantize_mx(out=codes[:].bitcast(FP8X4), scales=plane[:], in_=hid[:].rearrange("p c t -> p (c t)"))
+            result = ring.tile([P, PACK, STRIP], F32, name="result")
+            rounded = ring.tile([P, STRIP, PACK], BF16, name="rounded", align_bytes=64)
+            for b0 in range(0, STRIP, BLOCK):
+                cols = slice(b0, b0 + BLOCK)
+                bank = psum.tile([P, PACK, BLOCK], F32, name="bank")
+                for t in range(PACK):
+                    lhsT, lhsT_scale = weight_operands(w3, 0, t)
+                    nc.tensor.matmul_mx(
+                        out=bank[:, t, :], lhsT=lhsT, lhsT_scale=lhsT_scale,
+                        rhs=codes[:, cols].bitcast(FP8X4), rhs_scale=plane[:, cols], start=True, stop=True,
+                    )
+                nc.scalar.copy(out=rounded[:, cols, :], in_=bank[:].rearrange("p t c -> p c t"))
+                nc.scalar.copy(out=result[:, :, cols], in_=bank[:])
+            nc.sync.dma_start(out=out_rows[:, :, r0 : r0 + STRIP], in_=result[:])
+            return rounded
+
+        def hand_on(rounded, r0):
+            codes = ring.tile([P, STRIP], I32, name="out_codes", align_bytes=64)
+            nc.vector.quantize_mx(
+                out=codes[:].bitcast(FP8X4), scales=out_plane[:, r0 : r0 + STRIP],
+                in_=rounded[:].rearrange("p c t -> p (c t)"),
+            )
+            nc.sync.dma_start(out=out_words[:, r0 : r0 + STRIP], in_=codes[:])
+
+        later = []
+        c0 = 0
+        for n in CHUNKS:
+            terms = ring.tile([P, 2, PACK, n], F32, name="terms", bufs=2)
+            for t in range(PACK):
+                if c0 == 0:
+                    project(w1, t, y[t], 1.0)
+                    project(w2, t, negz[t], -1.0)
+                sim, negzl = fetch(c0, n, t)
+                now, later = later, []
+                for step in now:
+                    step()
+                diff = differences(c0, n, t, sim, negzl)
+                later.append(lambda t=t, diff=diff, terms=terms: clip(t, diff, terms))
+
+            def close(terms=terms, c0=c0, n=n):
+                for s0 in range(0, n, STRIP):
+                    def second(hid, r0):
+                        rounded = last_product(hid, r0)
+                        later.append(lambda: hand_on(rounded, r0))
+                    hid = hidden(terms, s0)
+                    later.append(lambda hid=hid, r0=c0 + s0, second=second: second(hid, r0))
+            later.append(close)
+            c0 = c0 + n
+        for unused in range(3):
+            now, later = later, []
+            for step in now:
+                step()
+
+        for q in range(QUADS):
+            queue = nc.sync if q % 2 == 0 else nc.scalar
+            queue.dma_start(
+                out=out_2[0, 4 * q : 4 * q + 4, :].bitcast(I32), in_=out_plane[32 * q : 32 * q + 4, :].bitcast(I32)
+            )

@@ -20,8 +20,16 @@ P = 128
 PACK = 4
 PASSES = K // (P * PACK)
 QUADS = 4
+XS_SPLIT = 1408
 SPARE = 16
 CHUNKS = (256, 512, 256)
+ZR_UNITS = (6, 7, 8, 9, 10, 11)
+PACE = 1
+DELAY = 3
+YR_UNITS = ()
+ROUND_V = 768
+Z_ON_VECTOR = 1
+RING = 3
 BLOCK = 128
 STRIP = 256
 
@@ -33,7 +41,7 @@ def tile_picked_ysegmrg_rng_po_kernel(
     nc = tc.nc
     with ExitStack() as ctx:
         keep = ctx.enter_context(tc.tile_pool(name="keep", bufs=1))
-        ring = ctx.enter_context(tc.tile_pool(name="ring", bufs=3))
+        ring = ctx.enter_context(tc.tile_pool(name="ring", bufs=RING))
         psum = ctx.enter_context(tc.psum_pool(name="psum", bufs=8))
 
         def load_scale_rows(queue, tile, scales):
@@ -48,78 +56,79 @@ def tile_picked_ysegmrg_rng_po_kernel(
             engine.memset(tile[:].bitcast(I32), 0)
             return tile
 
-        def load_words(queue, name, words):
-            passes = words.shape[0]
-            tile = keep.tile([P, passes, 2 * N], U8, name=name, align_bytes=64)
-            queue.dma_start(out=tile[:].bitcast(I32), in_=words.rearrange("g p b -> p g b").bitcast(I32))
-            return tile
-
-        def deal(name, raw_words, raw_scales):
-            passes = raw_words.shape[1]
-            words = keep.tile([P, passes, 2 * N], U8, name=name + "_words", align_bytes=64)
-            scales = keep.tile([P, passes, N], U8, name=name + "_scales", align_bytes=64)
-            nc.vector.tensor_copy(
-                out=words[:].bitcast(U16).rearrange("p g (t m) -> p g m t", t=PACK),
-                in_=raw_words[:].bitcast(U16).rearrange("p g (m t) -> p g m t", t=PACK),
-            )
-            nc.vector.tensor_copy(
-                out=scales[:].rearrange("p g (t m) -> p g m t", t=PACK),
-                in_=raw_scales[:].rearrange("p g (m t) -> p g m t", t=PACK),
-            )
-            return words, scales
+        def load_words(tile, words):
+            nc.sync.dma_start(out=tile[:].bitcast(I32), in_=words.rearrange("g p b -> p g b").bitcast(I32))
 
         def load_list(name, source):
             tile = keep.tile([P, source.shape[1]], U16, name=name)
             nc.sync.dma_start(tile[:], source)
             return tile
 
+        def deal_words(name, raw, tag):
+            words = keep.tile([P, raw.shape[1], 2 * N], U8, name=name, tag=tag, align_bytes=64)
+            nc.vector.tensor_copy(
+                out=words[:].bitcast(U16).rearrange("p g (t m) -> p g m t", t=PACK),
+                in_=raw[:].bitcast(U16).rearrange("p g (m t) -> p g m t", t=PACK),
+            )
+            return words
+
+        def deal_scales(name, passes):
+            scales = keep.tile([P, passes, N], U8, name=name, align_bytes=64)
+            nc.vector.tensor_copy(
+                out=scales[:].rearrange("p g (t m) -> p g m t", t=PACK),
+                in_=ws_raw[:, 0:passes, :].rearrange("p g (m t) -> p g m t", t=PACK),
+            )
+            return scales
+
         xs_raw = keep.tile([P, T], U8, name="xs_raw", align_bytes=64)
-        nc.vector.memset(xs_raw[:].bitcast(I32), 0)
-        w1s_raw = zeroed_plane(nc.vector, "w1s_raw", PASSES, N)
-        w2s_raw = zeroed_plane(nc.gpsimd, "w2s_raw", PASSES, N)
-        w3s_raw = zeroed_plane(nc.gpsimd, "w3s_raw", 1, N)
-        shifted = zeroed_plane(nc.vector, "shifted", 1, S)
+        nc.vector.memset(xs_raw[:, 0:XS_SPLIT].bitcast(I32), 0)
+        nc.gpsimd.memset(xs_raw[:, XS_SPLIT:T].bitcast(I32), 0)
+        ws_raw = zeroed_plane(nc.vector, "ws_raw", PASSES, N)
+        shifted = zeroed_plane(nc.gpsimd, "shifted", 1, S)
         for q in range(QUADS):
-            nc.scalar.dma_start(
+            nc.sync.dma_start(
                 out=xs_raw[32 * q : 32 * q + 4 * PASSES, :].bitcast(I32),
                 in_=x_scales[:, 4 * q : 4 * q + 4, :].bitcast(I32),
             )
-        load_scale_rows(nc.scalar, w1s_raw, w1_scales)
         picks = load_list("picks", offs)
-        w1w_raw = load_words(nc.sync, "w1w_raw", w1_words)
+        w1w_raw = keep.tile([P, PASSES, 2 * N], U8, name="w1w_raw")
+        load_words(w1w_raw, w1_words)
         left = load_list("left", l1)
-        right = load_list("right", r1)
-        xw_raw = [keep.tile([P, T], I32, name="xw_raw%d" % g, align_bytes=64) for g in range(PASSES)]
+        xw_raw = [keep.tile([P, T], I32, name="xw_raw%d" % g, tag="stage%d" % g, align_bytes=64) for g in range(PASSES)]
         nc.sync.dma_start(out=xw_raw[0][:], in_=x_words[0].rearrange("p c r -> p (c r)").bitcast(I32))
-        w2w_raw = load_words(nc.sync, "w2w_raw", w2_words)
+        load_scale_rows(nc.sync, ws_raw, w1_scales)
         nc.sync.dma_start(out=xw_raw[1][:], in_=x_words[1].rearrange("p c r -> p (c r)").bitcast(I32))
-        w3w_raw = load_words(nc.sync, "w3w_raw", w3_words)
-        load_scale_rows(nc.gpsimd, w2s_raw, w2_scales)
-        gain = keep.tile([P, PACK], F32, name="gain")
-        nc.gpsimd.dma_start(out=gain[:], in_=unit.rearrange("(p t) o -> p (t o)", t=PACK))
-        load_scale_rows(nc.gpsimd, w3s_raw, w3_scales)
+        w2w_raw = keep.tile([P, PASSES, 2 * N], U8, name="w2w_raw")
+        load_words(w2w_raw, w2_words)
+        right = load_list("right", r1)
 
         y = [keep.tile([P, S + SPARE], F32, name="y%d" % t) for t in range(PACK)]
         negz = [keep.tile([P, S + SPARE], F32, name="negz%d" % t) for t in range(PACK)]
         for window in y + negz:
-            nc.vector.memset(window[:, S:], 0.0)
+            nc.gpsimd.memset(window[:, S:], 0.0)
 
         packed = keep.tile([P, S], U8, name="packed", align_bytes=64)
         nc.vector.tensor_copy(out=packed[:], in_=xs_raw[:].indirect(picks[:]))
-        nc.sync.dma_start(out=shifted[0:112, 0, :].bitcast(I32), in_=packed[4:116, :].bitcast(I32))
+        nc.scalar.dma_start(out=shifted[0:112, 0, :].bitcast(I32), in_=packed[4:116, :].bitcast(I32))
         xq_scales = [packed[:], shifted[:, 0, :]]
+        w1 = (deal_words("w1_words", w1w_raw, "w1_words"), deal_scales("w1_scales", PASSES))
+        load_scale_rows(nc.sync, ws_raw, w2_scales)
         xq_words = [keep.tile([P, S], U32, name="xq_words%d" % g, align_bytes=64) for g in range(PASSES)]
-        nc.vector.tensor_copy(out=xq_words[0][:], in_=xw_raw[0][:].bitcast(U32).indirect(picks[:]))
-        w1 = deal("w1", w1w_raw, w1s_raw)
-        nc.vector.tensor_copy(out=xq_words[1][:], in_=xw_raw[1][:].bitcast(U32).indirect(picks[:]))
-        w2 = deal("w2", w2w_raw, w2s_raw)
-        w3 = deal("w3", w3w_raw, w3s_raw)
+        for g in range(PASSES):
+            nc.vector.tensor_copy(out=xq_words[g][:], in_=xw_raw[g][:].bitcast(U32).indirect(picks[:]))
+        w2 = (deal_words("w2_words", w2w_raw, "stage1"), deal_scales("w2_scales", PASSES))
+        gain = keep.tile([P, PACK], F32, name="gain", tag="stage0", align_bytes=64)
+        nc.sync.dma_start(out=gain[:], in_=unit.rearrange("(p t) o -> p (t o)", t=PACK))
+        w3w_raw = keep.tile([P, 1, 2 * N], U8, name="w3w_raw", tag="w2w_raw")
+        load_words(w3w_raw, w3_words)
+        load_scale_rows(nc.sync, ws_raw[:, 0:1, :], w3_scales)
+        w3 = (deal_words("w3_words", w3w_raw, "w3_words"), deal_scales("w3_scales", 1))
 
         def weight_operands(weight, g, t):
             words, scales = weight
             return words[:, g, 2 * P * t : 2 * P * (t + 1)].bitcast(FP4X4), scales[:, g, P * t : P * (t + 1)]
 
-        def project(weight, t, window, sign):
+        def project(weight, t, window, sign, on_vector):
             bank = psum.tile([P, S], F32, name="bank")
             for g in range(PASSES):
                 lhsT, lhsT_scale = weight_operands(weight, g, t)
@@ -128,35 +137,46 @@ def tile_picked_ysegmrg_rng_po_kernel(
                     rhs=xq_words[g][:].bitcast(FP8X4), rhs_scale=xq_scales[g],
                     start=(g == 0), stop=(g == PASSES - 1),
                 )
-            nc.scalar.activation(window[:, :S], bank[:], COPY, scale=sign)
+            if on_vector:
+                nc.vector.tensor_scalar(window[:, :S], bank[:], sign, None, ALU.mult)
+            else:
+                nc.scalar.activation(window[:, :S], bank[:], COPY, scale=sign)
 
         out_rows = out_0.rearrange("(p t) r -> p t r", t=PACK)
         out_words = out_1[0].rearrange("p c r -> p (c r)").bitcast(I32)
         out_plane = keep.tile([P, U], U8, name="out_plane", align_bytes=64)
 
-        def fetch(c0, n, t):
+        def fetch(c0, n, t, zr_on_scalar, yr_on_scalar):
             lo, hi = c0 // 16, (c0 + n) // 16
             yl = ring.tile([P, n], F32, name="yl")
             nc.scalar.activation(yl[:], y[t][:].indirect(left[:, lo:hi]), COPY)
+            if yr_on_scalar:
+                yr = ring.tile([P, n], F32, name="yr")
+                nc.scalar.activation(yr[:], y[t][:].indirect(right[:, lo:hi]), COPY)
             negzl = ring.tile([P, n], F32, name="negzl")
             nc.scalar.activation(negzl[:], negz[t][:].indirect(left[:, lo:hi]), COPY)
+            negzr = None
+            if zr_on_scalar:
+                negzr = ring.tile([P, n], F32, name="negzr")
+                nc.scalar.activation(negzr[:], negz[t][:].indirect(right[:, lo:hi]), COPY)
             sim = ring.tile([P, n], F32, name="sim")
-            nc.vector.tensor_tensor(sim[:], y[t][:].indirect(right[:, lo:hi]), yl[:], ALU.mult)
-            return sim, negzl
+            nc.vector.tensor_tensor(sim[:], yr[:] if yr_on_scalar else y[t][:].indirect(right[:, lo:hi]), yl[:], ALU.mult)
+            return sim, negzl, negzr
 
-        def differences(c0, n, t, sim, negzl):
+        def differences(c0, n, t, sim, negzl, negzr):
             lo, hi = c0 // 16, (c0 + n) // 16
             diff = ring.tile([P, 2, n], F32, name="diff")
-            nc.vector.tensor_tensor(diff[:, 0, :], negz[t][:].indirect(right[:, lo:hi]), sim[:], ALU.add)
+            source = negz[t][:].indirect(right[:, lo:hi]) if negzr is None else negzr[:]
+            nc.vector.tensor_tensor(diff[:, 0, :], source, sim[:], ALU.add)
             nc.vector.scalar_tensor_tensor(diff[:, 1, :], negzl[:], -1.0, sim[:], ALU.mult, ALU.subtract)
             return diff
 
         def clip(t, diff, terms):
             nc.vector.tensor_scalar(terms[:, :, t, :], diff[:], 0.0, gain[:, t : t + 1], ALU.max, ALU.mult)
 
-        def hidden(terms, s0):
-            cols = slice(s0, s0 + STRIP)
-            hid = ring.tile([P, STRIP, PACK], BF16, name="hid", align_bytes=64)
+        def hidden(terms, s0, width):
+            cols = slice(s0, s0 + width)
+            hid = ring.tile([P, width, PACK], BF16, name="hid", align_bytes=64)
             nc.vector.tensor_tensor(
                 hid[:].rearrange("p (c i) t -> p c t i", i=4),
                 terms[:, 0, :, cols].rearrange("p t (c i) -> p c t i", i=4),
@@ -165,13 +185,13 @@ def tile_picked_ysegmrg_rng_po_kernel(
             )
             return hid
 
-        def last_product(hid, r0):
-            codes = ring.tile([P, STRIP], U32, name="hid_codes", align_bytes=64)
-            plane = ring.tile([P, STRIP], U8, name="hid_plane", align_bytes=64)
+        def last_product(hid, r0, width, round_on_vector):
+            codes = ring.tile([P, width], U32, name="hid_codes", align_bytes=64)
+            plane = ring.tile([P, width], U8, name="hid_plane", align_bytes=64)
             nc.vector.quantize_mx(out=codes[:].bitcast(FP8X4), scales=plane[:], in_=hid[:].rearrange("p c t -> p (c t)"))
-            result = ring.tile([P, PACK, STRIP], F32, name="result")
-            rounded = ring.tile([P, STRIP, PACK], BF16, name="rounded", align_bytes=64)
-            for b0 in range(0, STRIP, BLOCK):
+            result = ring.tile([P, PACK, width], F32, name="result")
+            rounded = ring.tile([P, width, PACK], BF16, name="rounded", align_bytes=64)
+            for b0 in range(0, width, BLOCK):
                 cols = slice(b0, b0 + BLOCK)
                 bank = psum.tile([P, PACK, BLOCK], F32, name="bank")
                 for t in range(PACK):
@@ -180,46 +200,60 @@ def tile_picked_ysegmrg_rng_po_kernel(
                         out=bank[:, t, :], lhsT=lhsT, lhsT_scale=lhsT_scale,
                         rhs=codes[:, cols].bitcast(FP8X4), rhs_scale=plane[:, cols], start=True, stop=True,
                     )
-                nc.scalar.copy(out=rounded[:, cols, :], in_=bank[:].rearrange("p t c -> p c t"))
+                if round_on_vector:
+                    nc.vector.tensor_copy(out=rounded[:, cols, :], in_=bank[:].rearrange("p t c -> p c t"))
+                else:
+                    nc.scalar.copy(out=rounded[:, cols, :], in_=bank[:].rearrange("p t c -> p c t"))
                 nc.scalar.copy(out=result[:, :, cols], in_=bank[:])
-            nc.sync.dma_start(out=out_rows[:, :, r0 : r0 + STRIP], in_=result[:])
+            nc.sync.dma_start(out=out_rows[:, :, r0 : r0 + width], in_=result[:])
             return rounded
 
-        def hand_on(rounded, r0):
-            codes = ring.tile([P, STRIP], I32, name="out_codes", align_bytes=64)
+        def hand_on(rounded, r0, width):
+            codes = ring.tile([P, width], I32, name="out_codes", align_bytes=64)
             nc.vector.quantize_mx(
-                out=codes[:].bitcast(FP8X4), scales=out_plane[:, r0 : r0 + STRIP],
+                out=codes[:].bitcast(FP8X4), scales=out_plane[:, r0 : r0 + width],
                 in_=rounded[:].rearrange("p c t -> p (c t)"),
             )
-            nc.sync.dma_start(out=out_words[:, r0 : r0 + STRIP], in_=codes[:])
+            nc.sync.dma_start(out=out_words[:, r0 : r0 + width], in_=codes[:])
 
-        later = []
+        steps = {}
+
+        def after(at, step):
+            steps.setdefault(at, []).append(step)
+
+        def close(at, terms, c0, n):
+            last = c0 + n == U
+            width = BLOCK if last else STRIP
+            for k, s0 in enumerate(range(0, n, width)):
+                def first(k=k, s0=s0):
+                    hid = hidden(terms, s0, width)
+
+                    def second():
+                        rounded = last_product(hid, c0 + s0, width, c0 + s0 >= ROUND_V)
+                        after(at + k * PACE + 1 + DELAY, lambda: hand_on(rounded, c0 + s0, width))
+
+                    after(at + k * PACE + 1, second)
+
+                after(at + k * PACE, first)
+
         c0 = 0
+        u = 0
         for n in CHUNKS:
             terms = ring.tile([P, 2, PACK, n], F32, name="terms", bufs=2)
             for t in range(PACK):
                 if c0 == 0:
-                    project(w1, t, y[t], 1.0)
-                    project(w2, t, negz[t], -1.0)
-                sim, negzl = fetch(c0, n, t)
-                now, later = later, []
-                for step in now:
+                    project(w1, t, y[t], 1.0, False)
+                    project(w2, t, negz[t], -1.0, t < Z_ON_VECTOR)
+                sim, negzl, negzr = fetch(c0, n, t, u in ZR_UNITS, u in YR_UNITS)
+                for step in steps.pop(u, []):
                     step()
-                diff = differences(c0, n, t, sim, negzl)
-                later.append(lambda t=t, diff=diff, terms=terms: clip(t, diff, terms))
-
-            def close(terms=terms, c0=c0, n=n):
-                for s0 in range(0, n, STRIP):
-                    def second(hid, r0):
-                        rounded = last_product(hid, r0)
-                        later.append(lambda: hand_on(rounded, r0))
-                    hid = hidden(terms, s0)
-                    later.append(lambda hid=hid, r0=c0 + s0, second=second: second(hid, r0))
-            later.append(close)
+                diff = differences(c0, n, t, sim, negzl, negzr)
+                after(u + 1, lambda t=t, diff=diff, terms=terms: clip(t, diff, terms))
+                u = u + 1
+            close(u, terms, c0, n)
             c0 = c0 + n
-        for unused in range(3):
-            now, later = later, []
-            for step in now:
+        while steps:
+            for step in steps.pop(min(steps)):
                 step()
 
         for q in range(QUADS):

@@ -20,18 +20,19 @@ P = 128
 PACK = 4
 PASSES = K // (P * PACK)
 QUADS = 4
-XS_SPLIT = 1408
-SPARE = 16
-CHUNKS = (256, 512, 256)
-ZR_UNITS = (6, 7, 8, 9, 10, 11)
-PACE = 1
-DELAY = 3
-YR_UNITS = ()
-ROUND_V = 768
-Z_ON_VECTOR = 1
-RING = 3
-BLOCK = 128
+QUAD_ROWS = 4
+PER_COLUMN = 16
+RUN = 4
+
+CHUNKS = (768, 256)
+WINDOW = max(CHUNKS) + PER_COLUMN
 STRIP = 256
+BLOCK = 128
+ZR_FROM = 3
+YR_FROM = 4
+HAND_ON_LAG = 3
+XS_SPLIT = 1408
+RING = 3
 
 
 def tile_picked_ysegmrg_rng_po_kernel(
@@ -42,173 +43,169 @@ def tile_picked_ysegmrg_rng_po_kernel(
     with ExitStack() as ctx:
         keep = ctx.enter_context(tc.tile_pool(name="keep", bufs=1))
         ring = ctx.enter_context(tc.tile_pool(name="ring", bufs=RING))
-        psum = ctx.enter_context(tc.psum_pool(name="psum", bufs=8))
-
-        def load_scale_rows(queue, tile, scales):
-            for q in range(QUADS):
-                queue.dma_start(
-                    out=tile[32 * q : 32 * q + 4].bitcast(I32),
-                    in_=scales[:, 4 * q : 4 * q + 4, :].rearrange("g a c -> a g c").bitcast(I32),
-                )
-
-        def zeroed_plane(engine, name, passes, width):
-            tile = keep.tile([P, passes, width], U8, name=name, align_bytes=64)
-            engine.memset(tile[:].bitcast(I32), 0)
-            return tile
-
-        def load_words(tile, words):
-            nc.sync.dma_start(out=tile[:].bitcast(I32), in_=words.rearrange("g p b -> p g b").bitcast(I32))
+        psum = ctx.enter_context(tc.psum_pool(name="psum", bufs=4))
 
         def load_list(name, source):
             tile = keep.tile([P, source.shape[1]], U16, name=name)
             nc.sync.dma_start(tile[:], source)
             return tile
 
-        def deal_words(name, raw, tag):
-            words = keep.tile([P, raw.shape[1], 2 * N], U8, name=name, tag=tag, align_bytes=64)
-            nc.vector.tensor_copy(
-                out=words[:].bitcast(U16).rearrange("p g (t m) -> p g m t", t=PACK),
-                in_=raw[:].bitcast(U16).rearrange("p g (m t) -> p g m t", t=PACK),
-            )
-            return words
+        def load_words(staged, words):
+            nc.sync.dma_start(out=staged.bitcast(I32), in_=words.rearrange("g p b -> p g b").bitcast(I32))
 
-        def deal_scales(name, passes):
-            scales = keep.tile([P, passes, N], U8, name=name, align_bytes=64)
-            nc.vector.tensor_copy(
-                out=scales[:].rearrange("p g (t m) -> p g m t", t=PACK),
-                in_=ws_raw[:, 0:passes, :].rearrange("p g (m t) -> p g m t", t=PACK),
-            )
-            return scales
+        def load_scale_rows(staged, scales):
+            for q in range(QUADS):
+                rows = scales[:, QUAD_ROWS * q : QUAD_ROWS * (q + 1), :]
+                nc.sync.dma_start(
+                    out=staged[32 * q : 32 * q + QUAD_ROWS].bitcast(I32),
+                    in_=rows.rearrange("g a c -> a g c").bitcast(I32),
+                )
 
-        xs_raw = keep.tile([P, T], U8, name="xs_raw", align_bytes=64)
-        nc.vector.memset(xs_raw[:, 0:XS_SPLIT].bitcast(I32), 0)
-        nc.gpsimd.memset(xs_raw[:, XS_SPLIT:T].bitcast(I32), 0)
-        ws_raw = zeroed_plane(nc.vector, "ws_raw", PASSES, N)
-        shifted = zeroed_plane(nc.gpsimd, "shifted", 1, S)
+        def deal(name, staged_words, staged_scales, words_tag):
+            passes = staged_words.shape[1]
+            words = keep.tile([P, passes, 2 * N], U8, name=name + "_words", tag=words_tag, align_bytes=64)
+            nc.vector.tensor_copy(
+                out=words[:].bitcast(U16).rearrange("p g (t m) -> p g t m", t=PACK),
+                in_=staged_words.bitcast(U16).rearrange("p g (m t) -> p g t m", t=PACK),
+            )
+            scales = keep.tile([P, passes, N], U8, name=name + "_scales", align_bytes=64)
+            nc.vector.tensor_copy(
+                out=scales[:].rearrange("p g (t m) -> p g t m", t=PACK),
+                in_=staged_scales.rearrange("p g (m t) -> p g t m", t=PACK),
+            )
+            return words, scales
+
+        xs_table = keep.tile([P, T], U8, name="xs_table", align_bytes=64)
+        nc.vector.memset(xs_table[:, 0:XS_SPLIT].bitcast(I32), 0)
+        nc.gpsimd.memset(xs_table[:, XS_SPLIT:T].bitcast(I32), 0)
+        ws_staged = keep.tile([P, PASSES, N], U8, name="ws_staged", align_bytes=64)
+        nc.vector.memset(ws_staged[:].bitcast(I32), 0)
+        xq_plane1 = keep.tile([P, S], U8, name="xq_plane1", align_bytes=64)
+        nc.gpsimd.memset(xq_plane1[:].bitcast(I32), 0)
         for q in range(QUADS):
             nc.sync.dma_start(
-                out=xs_raw[32 * q : 32 * q + 4 * PASSES, :].bitcast(I32),
-                in_=x_scales[:, 4 * q : 4 * q + 4, :].bitcast(I32),
+                out=xs_table[32 * q : 32 * q + QUAD_ROWS * PASSES, :].bitcast(I32),
+                in_=x_scales[:, QUAD_ROWS * q : QUAD_ROWS * (q + 1), :].bitcast(I32),
             )
         picks = load_list("picks", offs)
-        w1w_raw = keep.tile([P, PASSES, 2 * N], U8, name="w1w_raw")
-        load_words(w1w_raw, w1_words)
+        w1w_staged = keep.tile([P, PASSES, 2 * N], U8, name="w1w_staged")
+        load_words(w1w_staged[:], w1_words)
         left = load_list("left", l1)
-        xw_raw = [keep.tile([P, T], I32, name="xw_raw%d" % g, tag="stage%d" % g, align_bytes=64) for g in range(PASSES)]
-        nc.sync.dma_start(out=xw_raw[0][:], in_=x_words[0].rearrange("p c r -> p (c r)").bitcast(I32))
-        load_scale_rows(nc.sync, ws_raw, w1_scales)
-        nc.sync.dma_start(out=xw_raw[1][:], in_=x_words[1].rearrange("p c r -> p (c r)").bitcast(I32))
-        w2w_raw = keep.tile([P, PASSES, 2 * N], U8, name="w2w_raw")
-        load_words(w2w_raw, w2_words)
+        xw_table = [
+            keep.tile([P, T], I32, name="xw_table%d" % g, tag="table%d" % g, align_bytes=64) for g in range(PASSES)
+        ]
+        nc.sync.dma_start(out=xw_table[0][:], in_=x_words[0].rearrange("p c r -> p (c r)").bitcast(I32))
+        load_scale_rows(ws_staged[:], w1_scales)
+        nc.sync.dma_start(out=xw_table[1][:], in_=x_words[1].rearrange("p c r -> p (c r)").bitcast(I32))
+        w2w_staged = keep.tile([P, PASSES, 2 * N], U8, name="w2w_staged")
+        load_words(w2w_staged[:], w2_words)
         right = load_list("right", r1)
+        gain = keep.tile([P, PACK], F32, name="gain")
+        nc.sync.dma_start(out=gain[:], in_=unit.rearrange("(p t) o -> p (t o)", t=PACK))
 
-        y = [keep.tile([P, S + SPARE], F32, name="y%d" % t) for t in range(PACK)]
-        negz = [keep.tile([P, S + SPARE], F32, name="negz%d" % t) for t in range(PACK)]
+        y = [keep.tile([P, WINDOW], F32, name="y%d" % t) for t in range(PACK)]
+        negz = [keep.tile([P, WINDOW], F32, name="negz%d" % t) for t in range(PACK)]
         for window in y + negz:
-            nc.gpsimd.memset(window[:, S:], 0.0)
+            nc.vector.memset(window[:, S:], 0.0)
 
-        packed = keep.tile([P, S], U8, name="packed", align_bytes=64)
-        nc.vector.tensor_copy(out=packed[:], in_=xs_raw[:].indirect(picks[:]))
-        nc.scalar.dma_start(out=shifted[0:112, 0, :].bitcast(I32), in_=packed[4:116, :].bitcast(I32))
-        xq_scales = [packed[:], shifted[:, 0, :]]
-        w1 = (deal_words("w1_words", w1w_raw, "w1_words"), deal_scales("w1_scales", PASSES))
-        load_scale_rows(nc.sync, ws_raw, w2_scales)
+        xq_plane0 = keep.tile([P, S], U8, name="xq_plane0", align_bytes=64)
+        nc.vector.tensor_copy(out=xq_plane0[:], in_=xs_table[:].indirect(picks[:]))
+        span = 32 * (QUADS - 1) + QUAD_ROWS
+        nc.scalar.dma_start(
+            out=xq_plane1[0:span, :].bitcast(I32), in_=xq_plane0[QUAD_ROWS : QUAD_ROWS + span, :].bitcast(I32)
+        )
+        xq_planes = [xq_plane0, xq_plane1]
+        w1 = deal("w1", w1w_staged[:], ws_staged[:], "w1_words")
+        load_scale_rows(ws_staged[:], w2_scales)
         xq_words = [keep.tile([P, S], U32, name="xq_words%d" % g, align_bytes=64) for g in range(PASSES)]
         for g in range(PASSES):
-            nc.vector.tensor_copy(out=xq_words[g][:], in_=xw_raw[g][:].bitcast(U32).indirect(picks[:]))
-        w2 = (deal_words("w2_words", w2w_raw, "stage1"), deal_scales("w2_scales", PASSES))
-        gain = keep.tile([P, PACK], F32, name="gain", tag="stage0", align_bytes=64)
-        nc.sync.dma_start(out=gain[:], in_=unit.rearrange("(p t) o -> p (t o)", t=PACK))
-        w3w_raw = keep.tile([P, 1, 2 * N], U8, name="w3w_raw", tag="w2w_raw")
-        load_words(w3w_raw, w3_words)
-        load_scale_rows(nc.sync, ws_raw[:, 0:1, :], w3_scales)
-        w3 = (deal_words("w3_words", w3w_raw, "w3_words"), deal_scales("w3_scales", 1))
+            nc.vector.tensor_copy(out=xq_words[g][:], in_=xw_table[g][:].bitcast(U32).indirect(picks[:]))
+        w2 = deal("w2", w2w_staged[:], ws_staged[:], "table1")
+        w3_staged = keep.tile([P, 1, 3 * N], U8, name="w3_staged", tag="table0", align_bytes=64)
+        w3w_staged, w3s_staged = w3_staged[:, :, : 2 * N], w3_staged[:, :, 2 * N :]
+        nc.gpsimd.memset(w3s_staged.bitcast(I32), 0)
+        load_words(w3w_staged, w3_words)
+        load_scale_rows(w3s_staged, w3_scales)
+        w3 = deal("w3", w3w_staged, w3s_staged, "w3_words")
 
-        def weight_operands(weight, g, t):
+        def stationary(weight, g, t):
             words, scales = weight
             return words[:, g, 2 * P * t : 2 * P * (t + 1)].bitcast(FP4X4), scales[:, g, P * t : P * (t + 1)]
 
-        def project(weight, t, window, sign, on_vector):
-            bank = psum.tile([P, S], F32, name="bank")
+        def project(weight, t):
+            bank = psum.tile([P, S], F32, name="projection_bank")
             for g in range(PASSES):
-                lhsT, lhsT_scale = weight_operands(weight, g, t)
+                lhsT, lhsT_scale = stationary(weight, g, t)
                 nc.tensor.matmul_mx(
                     out=bank[:], lhsT=lhsT, lhsT_scale=lhsT_scale,
-                    rhs=xq_words[g][:].bitcast(FP8X4), rhs_scale=xq_scales[g],
+                    rhs=xq_words[g][:].bitcast(FP8X4), rhs_scale=xq_planes[g][:],
                     start=(g == 0), stop=(g == PASSES - 1),
                 )
-            if on_vector:
-                nc.vector.tensor_scalar(window[:, :S], bank[:], sign, None, ALU.mult)
+            return bank
+
+        def make_windows(t):
+            nc.scalar.activation(y[t][:, :S], project(w1, t)[:], COPY, scale=1.0)
+            z_bank = project(w2, t)
+            if t == 0:
+                nc.vector.tensor_scalar(negz[t][:, :S], z_bank[:], -1.0, None, ALU.mult)
             else:
-                nc.scalar.activation(window[:, :S], bank[:], COPY, scale=sign)
+                nc.scalar.activation(negz[t][:, :S], z_bank[:], COPY, scale=-1.0)
+
+        def fetched(name, window, offsets):
+            tile = ring.tile([P, offsets.shape[1] * PER_COLUMN], F32, name=name)
+            nc.scalar.activation(tile[:], window[:].indirect(offsets), COPY)
+            return tile[:]
+
+        def side_by_side(tiles):
+            return tiles.rearrange("p t (c i) -> p c t i", i=RUN)
+
+        def interleaved(tile):
+            return tile.rearrange("p (c i) t -> p c t i", i=RUN)
 
         out_rows = out_0.rearrange("(p t) r -> p t r", t=PACK)
         out_words = out_1[0].rearrange("p c r -> p (c r)").bitcast(I32)
         out_plane = keep.tile([P, U], U8, name="out_plane", align_bytes=64)
 
-        def fetch(c0, n, t, zr_on_scalar, yr_on_scalar):
-            lo, hi = c0 // 16, (c0 + n) // 16
-            yl = ring.tile([P, n], F32, name="yl")
-            nc.scalar.activation(yl[:], y[t][:].indirect(left[:, lo:hi]), COPY)
-            if yr_on_scalar:
-                yr = ring.tile([P, n], F32, name="yr")
-                nc.scalar.activation(yr[:], y[t][:].indirect(right[:, lo:hi]), COPY)
-            negzl = ring.tile([P, n], F32, name="negzl")
-            nc.scalar.activation(negzl[:], negz[t][:].indirect(left[:, lo:hi]), COPY)
-            negzr = None
-            if zr_on_scalar:
-                negzr = ring.tile([P, n], F32, name="negzr")
-                nc.scalar.activation(negzr[:], negz[t][:].indirect(right[:, lo:hi]), COPY)
-            sim = ring.tile([P, n], F32, name="sim")
-            nc.vector.tensor_tensor(sim[:], yr[:] if yr_on_scalar else y[t][:].indirect(right[:, lo:hi]), yl[:], ALU.mult)
-            return sim, negzl, negzr
+        due = {}
 
-        def differences(c0, n, t, sim, negzl, negzr):
-            lo, hi = c0 // 16, (c0 + n) // 16
-            diff = ring.tile([P, 2, n], F32, name="diff")
-            source = negz[t][:].indirect(right[:, lo:hi]) if negzr is None else negzr[:]
-            nc.vector.tensor_tensor(diff[:, 0, :], source, sim[:], ALU.add)
-            nc.vector.scalar_tensor_tensor(diff[:, 1, :], negzl[:], -1.0, sim[:], ALU.mult, ALU.subtract)
-            return diff
+        def later(step, work):
+            due.setdefault(step, []).append(work)
 
         def clip(t, diff, terms):
             nc.vector.tensor_scalar(terms[:, :, t, :], diff[:], 0.0, gain[:, t : t + 1], ALU.max, ALU.mult)
 
-        def hidden(terms, s0, width):
-            cols = slice(s0, s0 + width)
-            hid = ring.tile([P, width, PACK], BF16, name="hid", align_bytes=64)
+        def add_terms(step, terms, cols, r0):
+            hid = ring.tile([P, cols.stop - cols.start, PACK], BF16, name="hid", align_bytes=64)
             nc.vector.tensor_tensor(
-                hid[:].rearrange("p (c i) t -> p c t i", i=4),
-                terms[:, 0, :, cols].rearrange("p t (c i) -> p c t i", i=4),
-                terms[:, 1, :, cols].rearrange("p t (c i) -> p c t i", i=4),
-                ALU.add,
+                interleaved(hid[:]), side_by_side(terms[:, 0, :, cols]), side_by_side(terms[:, 1, :, cols]), ALU.add
             )
-            return hid
+            later(step + 1, lambda: last_product(step + 1, hid, r0))
 
-        def last_product(hid, r0, width, round_on_vector):
+        def last_product(step, hid, r0):
+            width = hid.shape[1]
             codes = ring.tile([P, width], U32, name="hid_codes", align_bytes=64)
             plane = ring.tile([P, width], U8, name="hid_plane", align_bytes=64)
-            nc.vector.quantize_mx(out=codes[:].bitcast(FP8X4), scales=plane[:], in_=hid[:].rearrange("p c t -> p (c t)"))
+            nc.vector.quantize_mx(
+                out=codes[:].bitcast(FP8X4), scales=plane[:], in_=hid[:].rearrange("p c t -> p (c t)")
+            )
             result = ring.tile([P, PACK, width], F32, name="result")
-            rounded = ring.tile([P, width, PACK], BF16, name="rounded", align_bytes=64)
             for b0 in range(0, width, BLOCK):
-                cols = slice(b0, b0 + BLOCK)
-                bank = psum.tile([P, PACK, BLOCK], F32, name="bank")
+                block = slice(b0, b0 + BLOCK)
+                bank = psum.tile([P, PACK, BLOCK], F32, name="result_bank")
                 for t in range(PACK):
-                    lhsT, lhsT_scale = weight_operands(w3, 0, t)
+                    lhsT, lhsT_scale = stationary(w3, 0, t)
                     nc.tensor.matmul_mx(
                         out=bank[:, t, :], lhsT=lhsT, lhsT_scale=lhsT_scale,
-                        rhs=codes[:, cols].bitcast(FP8X4), rhs_scale=plane[:, cols], start=True, stop=True,
+                        rhs=codes[:, block].bitcast(FP8X4), rhs_scale=plane[:, block], start=True, stop=True,
                     )
-                if round_on_vector:
-                    nc.vector.tensor_copy(out=rounded[:, cols, :], in_=bank[:].rearrange("p t c -> p c t"))
-                else:
-                    nc.scalar.copy(out=rounded[:, cols, :], in_=bank[:].rearrange("p t c -> p c t"))
-                nc.scalar.copy(out=result[:, :, cols], in_=bank[:])
+                nc.scalar.copy(out=result[:, :, block], in_=bank[:])
             nc.sync.dma_start(out=out_rows[:, :, r0 : r0 + width], in_=result[:])
-            return rounded
+            later(step + HAND_ON_LAG, lambda: hand_on(result, r0))
 
-        def hand_on(rounded, r0, width):
+        def hand_on(result, r0):
+            width = result.shape[2]
+            rounded = ring.tile([P, width, PACK], BF16, name="rounded", align_bytes=64)
+            nc.vector.tensor_copy(out=interleaved(rounded[:]), in_=side_by_side(result[:]))
             codes = ring.tile([P, width], I32, name="out_codes", align_bytes=64)
             nc.vector.quantize_mx(
                 out=codes[:].bitcast(FP8X4), scales=out_plane[:, r0 : r0 + width],
@@ -216,48 +213,44 @@ def tile_picked_ysegmrg_rng_po_kernel(
             )
             nc.sync.dma_start(out=out_words[:, r0 : r0 + width], in_=codes[:])
 
-        steps = {}
-
-        def after(at, step):
-            steps.setdefault(at, []).append(step)
-
-        def close(at, terms, c0, n):
-            last = c0 + n == U
-            width = BLOCK if last else STRIP
-            for k, s0 in enumerate(range(0, n, width)):
-                def first(k=k, s0=s0):
-                    hid = hidden(terms, s0, width)
-
-                    def second():
-                        rounded = last_product(hid, c0 + s0, width, c0 + s0 >= ROUND_V)
-                        after(at + k * PACE + 1 + DELAY, lambda: hand_on(rounded, c0 + s0, width))
-
-                    after(at + k * PACE + 1, second)
-
-                after(at + k * PACE, first)
-
-        c0 = 0
-        u = 0
-        for n in CHUNKS:
-            terms = ring.tile([P, 2, PACK, n], F32, name="terms", bufs=2)
+        for chunk, n in enumerate(CHUNKS):
+            c0 = sum(CHUNKS[:chunk])
+            entries = slice(c0 // PER_COLUMN, (c0 + n) // PER_COLUMN)
+            terms = ring.tile([P, 2, PACK, n], F32, name="terms", bufs=len(CHUNKS))
             for t in range(PACK):
-                if c0 == 0:
-                    project(w1, t, y[t], 1.0, False)
-                    project(w2, t, negz[t], -1.0, t < Z_ON_VECTOR)
-                sim, negzl, negzr = fetch(c0, n, t, u in ZR_UNITS, u in YR_UNITS)
-                for step in steps.pop(u, []):
-                    step()
-                diff = differences(c0, n, t, sim, negzl, negzr)
-                after(u + 1, lambda t=t, diff=diff, terms=terms: clip(t, diff, terms))
-                u = u + 1
-            close(u, terms, c0, n)
-            c0 = c0 + n
-        while steps:
-            for step in steps.pop(min(steps)):
-                step()
+                step = PACK * chunk + t
+                if chunk == 0:
+                    make_windows(t)
+                yl = fetched("yl", y[t], left[:, entries])
+                if step >= YR_FROM:
+                    yr = fetched("yr", y[t], right[:, entries])
+                else:
+                    yr = y[t][:].indirect(right[:, entries])
+                negzl = fetched("negzl", negz[t], left[:, entries])
+                if step >= ZR_FROM:
+                    negzr = fetched("negzr", negz[t], right[:, entries])
+                else:
+                    negzr = negz[t][:].indirect(right[:, entries])
+                sim = ring.tile([P, n], F32, name="sim")
+                nc.vector.tensor_tensor(sim[:], yr, yl, ALU.mult)
+                for work in due.pop(step, []):
+                    work()
+                diff = ring.tile([P, 2, n], F32, name="diff")
+                nc.vector.tensor_tensor(diff[:, 0, :], negzr, sim[:], ALU.add)
+                nc.vector.scalar_tensor_tensor(diff[:, 1, :], negzl, -1.0, sim[:], ALU.mult, ALU.subtract)
+                later(step + 1, lambda t=t, diff=diff, terms=terms: clip(t, diff, terms))
+            width = BLOCK if chunk == len(CHUNKS) - 1 else STRIP
+            for k, s0 in enumerate(range(0, n, width)):
+                at = PACK * (chunk + 1) + k
+                cols = slice(s0, s0 + width)
+                later(at, lambda at=at, terms=terms, cols=cols, r0=c0 + s0: add_terms(at, terms, cols, r0))
+        while due:
+            for work in due.pop(min(due)):
+                work()
 
         for q in range(QUADS):
             queue = nc.sync if q % 2 == 0 else nc.scalar
             queue.dma_start(
-                out=out_2[0, 4 * q : 4 * q + 4, :].bitcast(I32), in_=out_plane[32 * q : 32 * q + 4, :].bitcast(I32)
+                out=out_2[0, QUAD_ROWS * q : QUAD_ROWS * (q + 1), :].bitcast(I32),
+                in_=out_plane[32 * q : 32 * q + QUAD_ROWS, :].bitcast(I32),
             )

from contextlib import ExitStack

import concourse.mybir as mybir

K, T, S, N, H, U = 1024, 2048, 512, 512, 512, 1024
FLOPS = 2 * (2 * K * N * S + H * N * U)

F32 = mybir.dt.float32
BF16 = mybir.dt.bfloat16
I32 = mybir.dt.int32
U32 = mybir.dt.uint32
U16 = mybir.dt.uint16
U8 = mybir.dt.uint8
FP8X4 = mybir.dt.float8_e4m3fn_x4
FP4X4 = mybir.dt.float4_e2m1fn_x4
ALU = mybir.AluOpType
COPY = mybir.ActivationFunctionType.Copy

P = 128
PACK = 4
PASSES = K // (P * PACK)
QUADS = 4
QUAD_ROWS = 4
PER_COLUMN = 16
RUN = 4

CHUNKS = (768, 256)
WINDOW = max(CHUNKS) + PER_COLUMN
STRIP = 256
BLOCK = 128
ZR_FROM = 3
YR_FROM = 4
HAND_ON_LAG = 3
XS_SPLIT = 1408
RING = 3


def tile_picked_ysegmrg_rng_po_kernel(
    tc, x_words, x_scales, w1_words, w1_scales, w2_words, w2_scales, unit, w3_words, w3_scales, offs, l1, r1,
    out_0, out_1, out_2,
):
    nc = tc.nc
    with ExitStack() as ctx:
        keep = ctx.enter_context(tc.tile_pool(name="keep", bufs=1))
        ring = ctx.enter_context(tc.tile_pool(name="ring", bufs=RING))
        psum = ctx.enter_context(tc.psum_pool(name="psum", bufs=4))

        def load_list(name, source):
            tile = keep.tile([P, source.shape[1]], U16, name=name)
            nc.sync.dma_start(tile[:], source)
            return tile

        def load_words(staged, words):
            nc.sync.dma_start(out=staged.bitcast(I32), in_=words.rearrange("g p b -> p g b").bitcast(I32))

        def load_scale_rows(staged, scales):
            for q in range(QUADS):
                rows = scales[:, QUAD_ROWS * q : QUAD_ROWS * (q + 1), :]
                nc.sync.dma_start(
                    out=staged[32 * q : 32 * q + QUAD_ROWS].bitcast(I32),
                    in_=rows.rearrange("g a c -> a g c").bitcast(I32),
                )

        def deal(name, staged_words, staged_scales, words_tag):
            passes = staged_words.shape[1]
            words = keep.tile([P, passes, 2 * N], U8, name=name + "_words", tag=words_tag, align_bytes=64)
            nc.vector.tensor_copy(
                out=words[:].bitcast(U16).rearrange("p g (t m) -> p g t m", t=PACK),
                in_=staged_words.bitcast(U16).rearrange("p g (m t) -> p g t m", t=PACK),
            )
            scales = keep.tile([P, passes, N], U8, name=name + "_scales", align_bytes=64)
            nc.vector.tensor_copy(
                out=scales[:].rearrange("p g (t m) -> p g t m", t=PACK),
                in_=staged_scales.rearrange("p g (m t) -> p g t m", t=PACK),
            )
            return words, scales

        xs_table = keep.tile([P, T], U8, name="xs_table", align_bytes=64)
        nc.vector.memset(xs_table[:, 0:XS_SPLIT].bitcast(I32), 0)
        nc.gpsimd.memset(xs_table[:, XS_SPLIT:T].bitcast(I32), 0)
        ws_staged = keep.tile([P, PASSES, N], U8, name="ws_staged", align_bytes=64)
        nc.vector.memset(ws_staged[:].bitcast(I32), 0)
        xq_plane1 = keep.tile([P, S], U8, name="xq_plane1", align_bytes=64)
        nc.gpsimd.memset(xq_plane1[:].bitcast(I32), 0)
        for q in range(QUADS):
            nc.sync.dma_start(
                out=xs_table[32 * q : 32 * q + QUAD_ROWS * PASSES, :].bitcast(I32),
                in_=x_scales[:, QUAD_ROWS * q : QUAD_ROWS * (q + 1), :].bitcast(I32),
            )
        picks = load_list("picks", offs)
        w1w_staged = keep.tile([P, PASSES, 2 * N], U8, name="w1w_staged")
        load_words(w1w_staged[:], w1_words)
        left = load_list("left", l1)
        xw_table = [
            keep.tile([P, T], I32, name="xw_table%d" % g, tag="table%d" % g, align_bytes=64) for g in range(PASSES)
        ]
        nc.sync.dma_start(out=xw_table[0][:], in_=x_words[0].rearrange("p c r -> p (c r)").bitcast(I32))
        load_scale_rows(ws_staged[:], w1_scales)
        nc.sync.dma_start(out=xw_table[1][:], in_=x_words[1].rearrange("p c r -> p (c r)").bitcast(I32))
        w2w_staged = keep.tile([P, PASSES, 2 * N], U8, name="w2w_staged")
        load_words(w2w_staged[:], w2_words)
        right = load_list("right", r1)
        gain = keep.tile([P, PACK], F32, name="gain")
        nc.sync.dma_start(out=gain[:], in_=unit.rearrange("(p t) o -> p (t o)", t=PACK))

        y = [keep.tile([P, WINDOW], F32, name="y%d" % t) for t in range(PACK)]
        negz = [keep.tile([P, WINDOW], F32, name="negz%d" % t) for t in range(PACK)]
        for window in y + negz:
            nc.vector.memset(window[:, S:], 0.0)

        xq_plane0 = keep.tile([P, S], U8, name="xq_plane0", align_bytes=64)
        nc.vector.tensor_copy(out=xq_plane0[:], in_=xs_table[:].indirect(picks[:]))
        span = 32 * (QUADS - 1) + QUAD_ROWS
        nc.scalar.dma_start(
            out=xq_plane1[0:span, :].bitcast(I32), in_=xq_plane0[QUAD_ROWS : QUAD_ROWS + span, :].bitcast(I32)
        )
        xq_planes = [xq_plane0, xq_plane1]
        w1 = deal("w1", w1w_staged[:], ws_staged[:], "w1_words")
        load_scale_rows(ws_staged[:], w2_scales)
        xq_words = [keep.tile([P, S], U32, name="xq_words%d" % g, align_bytes=64) for g in range(PASSES)]
        for g in range(PASSES):
            nc.vector.tensor_copy(out=xq_words[g][:], in_=xw_table[g][:].bitcast(U32).indirect(picks[:]))
        w2 = deal("w2", w2w_staged[:], ws_staged[:], "table1")
        w3_staged = keep.tile([P, 1, 3 * N], U8, name="w3_staged", tag="table0", align_bytes=64)
        w3w_staged, w3s_staged = w3_staged[:, :, : 2 * N], w3_staged[:, :, 2 * N :]
        nc.gpsimd.memset(w3s_staged.bitcast(I32), 0)
        load_words(w3w_staged, w3_words)
        load_scale_rows(w3s_staged, w3_scales)
        w3 = deal("w3", w3w_staged, w3s_staged, "w3_words")

        def stationary(weight, g, t):
            words, scales = weight
            return words[:, g, 2 * P * t : 2 * P * (t + 1)].bitcast(FP4X4), scales[:, g, P * t : P * (t + 1)]

        def project(weight, t):
            bank = psum.tile([P, S], F32, name="projection_bank")
            for g in range(PASSES):
                lhsT, lhsT_scale = stationary(weight, g, t)
                nc.tensor.matmul_mx(
                    out=bank[:], lhsT=lhsT, lhsT_scale=lhsT_scale,
                    rhs=xq_words[g][:].bitcast(FP8X4), rhs_scale=xq_planes[g][:],
                    start=(g == 0), stop=(g == PASSES - 1),
                )
            return bank

        def make_windows(t):
            nc.scalar.activation(y[t][:, :S], project(w1, t)[:], COPY, scale=1.0)
            z_bank = project(w2, t)
            if t == 0:
                nc.vector.tensor_scalar(negz[t][:, :S], z_bank[:], -1.0, None, ALU.mult)
            else:
                nc.scalar.activation(negz[t][:, :S], z_bank[:], COPY, scale=-1.0)

        def fetched(name, window, offsets):
            tile = ring.tile([P, offsets.shape[1] * PER_COLUMN], F32, name=name)
            nc.scalar.activation(tile[:], window[:].indirect(offsets), COPY)
            return tile[:]

        def side_by_side(tiles):
            return tiles.rearrange("p t (c i) -> p c t i", i=RUN)

        def interleaved(tile):
            return tile.rearrange("p (c i) t -> p c t i", i=RUN)

        out_rows = out_0.rearrange("(p t) r -> p t r", t=PACK)
        out_words = out_1[0].rearrange("p c r -> p (c r)").bitcast(I32)
        out_plane = keep.tile([P, U], U8, name="out_plane", align_bytes=64)

        due = {}

        def later(step, work):
            due.setdefault(step, []).append(work)

        def clip(t, diff, terms):
            nc.vector.tensor_scalar(terms[:, :, t, :], diff[:], 0.0, gain[:, t : t + 1], ALU.max, ALU.mult)

        def add_terms(step, terms, cols, r0):
            hid = ring.tile([P, cols.stop - cols.start, PACK], BF16, name="hid", align_bytes=64)
            nc.vector.tensor_tensor(
                interleaved(hid[:]), side_by_side(terms[:, 0, :, cols]), side_by_side(terms[:, 1, :, cols]), ALU.add
            )
            later(step + 1, lambda: last_product(step + 1, hid, r0))

        def last_product(step, hid, r0):
            width = hid.shape[1]
            codes = ring.tile([P, width], U32, name="hid_codes", align_bytes=64)
            plane = ring.tile([P, width], U8, name="hid_plane", align_bytes=64)
            nc.vector.quantize_mx(
                out=codes[:].bitcast(FP8X4), scales=plane[:], in_=hid[:].rearrange("p c t -> p (c t)")
            )
            result = ring.tile([P, PACK, width], F32, name="result")
            for b0 in range(0, width, BLOCK):
                block = slice(b0, b0 + BLOCK)
                bank = psum.tile([P, PACK, BLOCK], F32, name="result_bank")
                for t in range(PACK):
                    lhsT, lhsT_scale = stationary(w3, 0, t)
                    nc.tensor.matmul_mx(
                        out=bank[:, t, :], lhsT=lhsT, lhsT_scale=lhsT_scale,
                        rhs=codes[:, block].bitcast(FP8X4), rhs_scale=plane[:, block], start=True, stop=True,
                    )
                nc.scalar.copy(out=result[:, :, block], in_=bank[:])
            nc.sync.dma_start(out=out_rows[:, :, r0 : r0 + width], in_=result[:])
            later(step + HAND_ON_LAG, lambda: hand_on(result, r0))

        def hand_on(result, r0):
            width = result.shape[2]
            rounded = ring.tile([P, width, PACK], BF16, name="rounded", align_bytes=64)
            nc.vector.tensor_copy(out=interleaved(rounded[:]), in_=side_by_side(result[:]))
            codes = ring.tile([P, width], I32, name="out_codes", align_bytes=64)
            nc.vector.quantize_mx(
                out=codes[:].bitcast(FP8X4), scales=out_plane[:, r0 : r0 + width],
                in_=rounded[:].rearrange("p c t -> p (c t)"),
            )
            nc.sync.dma_start(out=out_words[:, r0 : r0 + width], in_=codes[:])

        for chunk, n in enumerate(CHUNKS):
            c0 = sum(CHUNKS[:chunk])
            entries = slice(c0 // PER_COLUMN, (c0 + n) // PER_COLUMN)
            terms = ring.tile([P, 2, PACK, n], F32, name="terms", bufs=len(CHUNKS))
            for t in range(PACK):
                step = PACK * chunk + t
                if chunk == 0:
                    make_windows(t)
                yl = fetched("yl", y[t], left[:, entries])
                if step >= YR_FROM:
                    yr = fetched("yr", y[t], right[:, entries])
                else:
                    yr = y[t][:].indirect(right[:, entries])
                negzl = fetched("negzl", negz[t], left[:, entries])
                if step >= ZR_FROM:
                    negzr = fetched("negzr", negz[t], right[:, entries])
                else:
                    negzr = negz[t][:].indirect(right[:, entries])
                sim = ring.tile([P, n], F32, name="sim")
                nc.vector.tensor_tensor(sim[:], yr, yl, ALU.mult)
                for work in due.pop(step, []):
                    work()
                diff = ring.tile([P, 2, n], F32, name="diff")
                nc.vector.tensor_tensor(diff[:, 0, :], negzr, sim[:], ALU.add)
                nc.vector.scalar_tensor_tensor(diff[:, 1, :], negzl, -1.0, sim[:], ALU.mult, ALU.subtract)
                later(step + 1, lambda t=t, diff=diff, terms=terms: clip(t, diff, terms))
            width = BLOCK if chunk == len(CHUNKS) - 1 else STRIP
            for k, s0 in enumerate(range(0, n, width)):
                at = PACK * (chunk + 1) + k
                cols = slice(s0, s0 + width)
                later(at, lambda at=at, terms=terms, cols=cols, r0=c0 + s0: add_terms(at, terms, cols, r0))
        while due:
            for work in due.pop(min(due)):
                work()

        for q in range(QUADS):
            queue = nc.sync if q % 2 == 0 else nc.scalar
            queue.dma_start(
                out=out_2[0, QUAD_ROWS * q : QUAD_ROWS * (q + 1), :].bitcast(I32),
                in_=out_plane[32 * q : 32 * q + QUAD_ROWS, :].bitcast(I32),
            )
